import numpy as np
import ml_dtypes


def mxq(x, axis, fmt="e4m3"):
    dtype, down = {"e4m3": (ml_dtypes.float8_e4m3fn, 7), "e5m2": (ml_dtypes.float8_e5m2, 14)}[fmt]
    v = np.moveaxis(np.asarray(x, np.float32).astype(ml_dtypes.bfloat16).astype(np.float64), axis, -1)
    blocks = v.reshape(v.shape[:-1] + (-1, 32))
    amax = np.abs(blocks).max(-1, keepdims=True)
    byte = np.maximum(np.where(amax > 0, np.frexp(amax)[1] - 1 + 127, 0) - down, 1)
    scale = np.exp2(byte - 127.0)
    codes = (blocks / scale).astype(np.float32).astype(dtype).astype(np.float64)
    return np.moveaxis((codes * scale).reshape(v.shape), -1, axis)


WIDE = False


def mx_kscale(k):
    if not WIDE:
        return np.ones(k)
    levels = np.array([10, -10, 5, -5, 0])
    if k % 512:
        return np.exp2(np.random.permutation(np.resize(levels, k // 32))).repeat(32)
    a = np.empty((k // 512, 16))
    for p in range(k // 512):
        a[p, :8] = np.random.permutation(np.resize(levels, 8))
        for g in range(8):
            far = levels[np.abs(levels - a[p, g]) >= 10]
            a[p, g + 8] = far[np.random.randint(len(far))]
    return np.exp2(a.ravel()).repeat(32)


def f64(x):
    return np.asarray(x).astype(np.float64)


def striped(idx):
    return np.tile(np.asarray(idx).reshape(-1, 16).T, (8, 1)).astype(np.uint16)


def unstriped(offs):
    return offs[:16].T.reshape(-1).astype(np.int64)


E2M1 = np.array([0.0, 0.5, 1.0, 1.5, 2.0, 3.0, 4.0, 6.0, -0.0, -0.5, -1.0, -1.5, -2.0, -3.0, -4.0, -6.0])


def pack_weight(w, fmt):
    k, n = w.shape
    w = f64(np.asarray(w, np.float32).astype(ml_dtypes.bfloat16)).reshape(k // 32, 32, n)
    amax = np.abs(w).max(1)
    if fmt == "e4m3":
        byte = np.frexp(amax)[1] - 1 + 127 - 7
    else:
        mant, ex = np.frexp(amax / 6.0)
        byte = np.where(mant > 0.5, ex, ex - 1) + 127
    byte = np.clip(np.where(amax > 0, byte, 1), 1, 254)
    scaled = (w * np.exp2(127.0 - byte)[:, None, :]).reshape(k, n).astype(np.float32)
    by_word = np.ascontiguousarray(scaled.reshape(k // 512, 128, 4, n).transpose(0, 1, 3, 2))
    if fmt == "e4m3":
        words = by_word.astype(ml_dtypes.float8_e4m3fn).view(np.uint8)
    else:
        c = by_word.astype(ml_dtypes.float4_e2m1fn).view(np.uint8) & 0xF
        words = (c[..., 0::2] | (c[..., 1::2] << 4)).reshape(k // 512, 128, 2 * n)
    return np.ascontiguousarray(words), np.ascontiguousarray(byte.astype(np.uint8).reshape(k // 512, 16, n))


def unpack_weight(words, scales, fmt):
    g, _, n = scales.shape
    words = np.ascontiguousarray(words).reshape(g, 128, n, -1)
    if fmt == "e4m3":
        vals = words.view(ml_dtypes.float8_e4m3fn).astype(np.float64)
    else:
        nib = np.empty((g, 128, n, 4), np.uint8)
        nib[..., 0::2] = words & 0xF
        nib[..., 1::2] = words >> 4
        vals = E2M1[nib]
    vals = vals * np.repeat(np.exp2(scales.astype(np.float64) - 127.0), 8, axis=1)[..., None]
    return vals.transpose(0, 1, 3, 2).reshape(g * 512, n)


K, T, J, N = 1024, 1024, 512, 512


def setup_inputs():
    n = np.random.standard_normal
    idx = np.random.permutation(T)[:J]
    fk = mx_kscale(K)
    xtp = pack_weight(n((K, T)) / fk[:, None], "e4m3")
    return {
        "xt_words": xtp[0],
        "xt_scales": xtp[1],
        "w": (n((K, N)) * 1 / np.sqrt(K) * fk[:, None]).astype(np.float32),
        "th": (np.random.uniform(0.2, 0.8, (N, 1))).astype(np.float32),
        "page": (1.0 * n((N, T))).astype(np.float32),
        "offs": striped(idx),
    }


def reference(xt_words, xt_scales, w, th, page, offs):
    idx = unstriped(offs)
    xtu = unpack_weight(xt_words, xt_scales, "e4m3")
    wq = mxq(f64(w), 0, "e4m3")
    xtidxg = xtu[:, idx]
    z = wq.T @ xtidxg
    d = z - f64(page)[:, idx]
    e = np.maximum(d - f64(th), 0.0) - np.maximum(0.0 - d - f64(th), 0.0)
    p = np.zeros((N, T))
    p[:, idx] = e
    y = 0.5 * f64(page) + p
    return y

from contextlib import ExitStack

import concourse.mybir as mybir

K, T, J, N = 1024, 1024, 512, 512
FLOPS = 2 * K * J * N

F32 = mybir.dt.float32
BF16 = mybir.dt.bfloat16
I32 = mybir.dt.int32
U32 = mybir.dt.uint32
U16 = mybir.dt.uint16
U8 = mybir.dt.uint8
FP8X4 = mybir.dt.float8_e4m3fn_x4
ALU = mybir.AluOpType
COPY = mybir.ActivationFunctionType.Copy

P = 128
PACK = 4
PASSES = K // (P * PACK)
TILES = N // P
HALF = J // 2


def tile_list_shrunk_towards_page_kernel(tc, xt_words, xt_scales, w, th, page, offs, out):
    nc = tc.nc
    with ExitStack() as ctx:
        keep = ctx.enter_context(tc.tile_pool(name="keep", bufs=1))
        psum = ctx.enter_context(tc.psum_pool(name="psum", bufs=1))

        def tiles(name, shape, dtype, count):
            return [keep.tile(shape, dtype, name="%s%d" % (name, i), align_bytes=64) for i in range(count)]

        offsets = keep.tile([P, J // 16], U16, name="offsets")
        words = tiles("words", [P, T], U32, PASSES)
        scales = keep.tile([P, T], U8, name="scales", align_bytes=64)
        picked_words = tiles("picked_words", [P, J], U32, PASSES)
        picked_scales = keep.tile([P, J], U8, name="picked_scales", align_bytes=64)
        w_raw = [tiles("w_raw%d_" % m, [P, PACK, P], F32, PASSES) for m in range(TILES)]
        w_bf = tiles("w_bf", [P, PASSES, P, PACK], BF16, TILES)
        w_codes = tiles("w_codes", [P, PASSES * P], U32, TILES)
        w_scales = tiles("w_scales", [P, PASSES * P], U8, TILES)
        pages = tiles("pages", [P, T], F32, TILES)
        picked_page = tiles("picked_page", [P, J], F32, TILES)
        work = tiles("work", [P, T], F32, TILES + 1)
        diff = [work[m][:, 0:J] for m in range(TILES)]
        low = [work[m][:, J : 2 * J] for m in range(TILES)]
        high = tiles("high", [P, J], F32, TILES)
        placed = tiles("placed", [P, T], F32, TILES)
        result = work[1:]
        th_pos = keep.tile([P, TILES], F32, name="th_pos")
        th_neg = keep.tile([P, TILES], F32, name="th_neg")
        acc = {}

        def listed(lo, hi):
            return offsets[:, lo // 16 : hi // 16]

        def load_words(a):
            nc.sync.dma_start(out=words[a][:].bitcast(I32), in_=xt_words[a].rearrange("p c r -> p (c r)").bitcast(I32))

        def load_w(m, a):
            rows = w[a * P * PACK : (a + 1) * P * PACK, m * P : (m + 1) * P]
            nc.sync.dma_start(out=w_raw[m][a][:], in_=rows.rearrange("(p j) n -> p j n", j=PACK))

        def load_page(m):
            nc.sync.dma_start(out=pages[m][:], in_=page[m * P : (m + 1) * P, :])

        def pick_words(a, lo, hi):
            nc.vector.tensor_copy(picked_words[a][:, lo:hi], words[a][:].indirect(listed(lo, hi)))

        def interleave(m, a, on_scalar):
            dst = w_bf[m][:, a].rearrange("p (c i) t -> p c t i", i=4)
            src = w_raw[m][a][:].rearrange("p t (c i) -> p c t i", i=4)
            if on_scalar:
                nc.scalar.copy(dst, src)
            else:
                nc.vector.tensor_copy(dst, src)

        def quantize(m):
            nc.vector.quantize_mx(
                out=w_codes[m][:].bitcast(FP8X4),
                scales=w_scales[m][:],
                in_=w_bf[m][:].rearrange("p a n t -> p (a n t)"),
            )

        def multiply(m, lo, hi):
            acc[m, lo] = psum.tile([P, hi - lo], F32, name="acc%d_%d" % (m, lo))
            for a in range(PASSES):
                cols = slice(a * P, (a + 1) * P)
                nc.tensor.matmul_mx(
                    out=acc[m, lo][:],
                    lhsT=w_codes[m][:, cols].bitcast(FP8X4),
                    lhsT_scale=w_scales[m][:, cols],
                    rhs=picked_words[a][:, lo:hi].bitcast(FP8X4),
                    rhs_scale=picked_scales[4 * a : P, lo:hi],
                    start=(a == 0),
                    stop=(a == PASSES - 1),
                )

        def pick_page(m, lo, hi, on_scalar):
            window = pages[m][:].indirect(listed(lo, hi))
            if on_scalar:
                nc.scalar.activation(picked_page[m][:, lo:hi], window, COPY)
            else:
                nc.vector.tensor_copy(picked_page[m][:, lo:hi], window)

        def difference(m, lo, hi):
            nc.vector.tensor_tensor(diff[m][:, lo:hi], acc[m, lo][:], picked_page[m][:, lo:hi], ALU.subtract)

        def low_part(m, lo, hi):
            nc.vector.tensor_scalar(low[m][:, lo:hi], diff[m][:, lo:hi], th_neg[:, m : m + 1], None, ALU.min)

        def high_part(m, lo, hi):
            nc.vector.tensor_scalar(high[m][:, lo:hi], diff[m][:, lo:hi], th_pos[:, m : m + 1], None, ALU.max)

        def excess(m, lo, hi):
            nc.vector.scalar_tensor_tensor(
                high[m][:, lo:hi], diff[m][:, lo:hi], th_pos[:, m : m + 1], low[m][:, lo:hi], ALU.max, ALU.add
            )

        def place_scalar(m, lo, hi):
            nc.scalar.activation(placed[m][:].indirect(listed(lo, hi)), high[m][:, lo:hi], COPY)

        def place_vector(m, lo, hi):
            nc.vector.tensor_tensor(
                placed[m][:].indirect(listed(lo, hi)), high[m][:, lo:hi], low[m][:, lo:hi], ALU.add
            )

        def finish(m, lo, hi):
            nc.vector.scalar_tensor_tensor(
                result[m][:, lo:hi], pages[m][:, lo:hi], 0.5, placed[m][:, lo:hi], ALU.mult, ALU.add
            )
            nc.sync.dma_start(out=out[m * P : (m + 1) * P, lo:hi], in_=result[m][:, lo:hi])

        nc.vector.memset(scales[:].bitcast(I32), 0)
        nc.sync.dma_start(offsets[:], offs)
        for q in range(4):
            nc.scalar.dma_start(
                out=scales[32 * q : 32 * q + 8, :].bitcast(I32),
                in_=xt_scales[:, 4 * q : 4 * q + 4, :].bitcast(I32),
            )
        load_words(0)
        with nc.allow_non_contiguous_dma(reason="one threshold a partition"):
            nc.scalar.dma_start(out=th_pos[:], in_=th.rearrange("(m p) o -> p (m o)", p=P))
        load_w(0, 0)
        load_w(0, 1)
        load_words(1)
        load_page(0)
        for m in range(1, TILES):
            load_page(m)
            load_w(m, 0)
            load_w(m, 1)
        for m in range(TILES):
            nc.vector.memset(placed[m][:], 0.0)
        nc.scalar.mul(th_neg[:], th_pos[:], -1.0)

        nc.vector.tensor_copy(picked_scales[:], scales[:].indirect(offsets[:]))
        pick_words(0, 0, J)
        interleave(0, 0, True)
        interleave(0, 1, True)
        quantize(0)
        for lo in (0, HALF):
            pick_words(1, lo, lo + HALF)
            multiply(0, lo, lo + HALF)
        pick_page(0, 0, HALF, True)
        pick_page(0, HALF, J, False)
        for lo in (0, HALF):
            difference(0, lo, lo + HALF)
            low_part(0, lo, lo + HALF)
            excess(0, lo, lo + HALF)
            place_scalar(0, lo, lo + HALF)
        for m in (1, 2, 3):
            interleave(m, 0, False)
            interleave(m, 1, False)
            quantize(m)
            multiply(m, 0, J)
            pick_page(m, 0, J, True)
            difference(m, 0, J)
            low_part(m, 0, J)
            if m < 3:
                excess(m, 0, J)
                place_scalar(m, 0, HALF)
                place_scalar(m, HALF, J)
        high_part(3, 0, HALF)
        excess(3, HALF, J)
        place_vector(3, 0, HALF)
        place_scalar(3, HALF, J)
        for m in range(3):
            finish(m, 0, T)
        finish(3, 0, T // 2)
        finish(3, T // 2, T)
